import numpy as np
import ml_dtypes


def mxq(x, axis, fmt="e4m3"):
    dtype, down = {"e4m3": (ml_dtypes.float8_e4m3fn, 7), "e5m2": (ml_dtypes.float8_e5m2, 14)}[fmt]
    v = np.moveaxis(np.asarray(x, np.float32).astype(ml_dtypes.bfloat16).astype(np.float64), axis, -1)
    blocks = v.reshape(v.shape[:-1] + (-1, 32))
    amax = np.abs(blocks).max(-1, keepdims=True)
    byte = np.maximum(np.where(amax > 0, np.frexp(amax)[1] - 1 + 127, 0) - down, 1)
    scale = np.exp2(byte - 127.0)
    codes = (blocks / scale).astype(np.float32).astype(dtype).astype(np.float64)
    return np.moveaxis((codes * scale).reshape(v.shape), -1, axis)


WIDE = False


def mx_kscale(k):
    if not WIDE:
        return np.ones(k)
    levels = np.array([10, -10, 5, -5, 0])
    if k % 512:
        return np.exp2(np.random.permutation(np.resize(levels, k // 32))).repeat(32)
    a = np.empty((k // 512, 16))
    for p in range(k // 512):
        a[p, :8] = np.random.permutation(np.resize(levels, 8))
        for g in range(8):
            far = levels[np.abs(levels - a[p, g]) >= 10]
            a[p, g + 8] = far[np.random.randint(len(far))]
    return np.exp2(a.ravel()).repeat(32)


def f64(x):
    return np.asarray(x).astype(np.float64)


def striped(idx):
    return np.tile(np.asarray(idx).reshape(-1, 16).T, (8, 1)).astype(np.uint16)


def unstriped(offs):
    return offs[:16].T.reshape(-1).astype(np.int64)


E2M1 = np.array([0.0, 0.5, 1.0, 1.5, 2.0, 3.0, 4.0, 6.0, -0.0, -0.5, -1.0, -1.5, -2.0, -3.0, -4.0, -6.0])


def pack_weight(w, fmt):
    k, n = w.shape
    w = f64(np.asarray(w, np.float32).astype(ml_dtypes.bfloat16)).reshape(k // 32, 32, n)
    amax = np.abs(w).max(1)
    if fmt == "e4m3":
        byte = np.frexp(amax)[1] - 1 + 127 - 7
    else:
        mant, ex = np.frexp(amax / 6.0)
        byte = np.where(mant > 0.5, ex, ex - 1) + 127
    byte = np.clip(np.where(amax > 0, byte, 1), 1, 254)
    scaled = (w * np.exp2(127.0 - byte)[:, None, :]).reshape(k, n).astype(np.float32)
    by_word = np.ascontiguousarray(scaled.reshape(k // 512, 128, 4, n).transpose(0, 1, 3, 2))
    if fmt == "e4m3":
        words = by_word.astype(ml_dtypes.float8_e4m3fn).view(np.uint8)
    else:
        c = by_word.astype(ml_dtypes.float4_e2m1fn).view(np.uint8) & 0xF
        words = (c[..., 0::2] | (c[..., 1::2] << 4)).reshape(k // 512, 128, 2 * n)
    return np.ascontiguousarray(words), np.ascontiguousarray(byte.astype(np.uint8).reshape(k // 512, 16, n))


def unpack_weight(words, scales, fmt):
    g, _, n = scales.shape
    words = np.ascontiguousarray(words).reshape(g, 128, n, -1)
    if fmt == "e4m3":
        vals = words.view(ml_dtypes.float8_e4m3fn).astype(np.float64)
    else:
        nib = np.empty((g, 128, n, 4), np.uint8)
        nib[..., 0::2] = words & 0xF
        nib[..., 1::2] = words >> 4
        vals = E2M1[nib]
    vals = vals * np.repeat(np.exp2(scales.astype(np.float64) - 127.0), 8, axis=1)[..., None]
    return vals.transpose(0, 1, 3, 2).reshape(g * 512, n)


def bf(x):
    return np.asarray(x, np.float32).astype(ml_dtypes.bfloat16)


def planes(Y):
    r, m = Y.shape
    b = f64(bf(Y)).reshape(r // 32, 32, m)
    amax = np.abs(b).max(1)
    byte = np.clip(np.where(amax > 0, np.frexp(amax)[1] - 1 + 127 - 7, 1), 1, 254)
    codes = (b * np.exp2(127.0 - byte)[:, None, :]).reshape(r, m).astype(np.float32).astype(ml_dtypes.float8_e4m3fn).view(np.uint8)
    words = codes.reshape(r // 512, 128, 4, m).transpose(0, 1, 3, 2)
    return np.ascontiguousarray(words), np.ascontiguousarray(byte.astype(np.uint8).reshape(r // 512, 16, m))


D, T, I, Q, E, V, G, K = 512, 2048, 512, 256, 512, 32, 64, 32


def setup_inputs():
    n = np.random.standard_normal
    idx = np.random.permutation(T)[:I]
    fd = mx_kscale(D)
    fi = mx_kscale(I)
    ti = np.ones(T)
    ti[idx] = fi
    keysp = pack_weight(n((D, T)) / fd[:, None], "e2m1")
    return {
        "query": (n((D, Q)) * 1.0 / np.sqrt(D) * fd[:, None]).astype(np.float32),
        "keys_words": keysp[0],
        "keys_scales": keysp[1],
        "lam": (np.random.uniform(0.7, 1.5, (1, Q))).astype(np.float32),
        "bar": (np.random.uniform(0.6, 1.0, (Q, 1))).astype(np.float32),
        "reserve": (np.random.uniform(20.0, 80.0, (Q, 1))).astype(np.float32),
        "os": (np.random.uniform(4.0, 16.0, (1, I)) * fi).astype(np.float32),
        "vals": (n((E, T)) / ti).astype(np.float32),
        "hold": (np.random.uniform(0.4, 1.0, (1, Q))).astype(np.float32),
        "offs": striped(idx),
    }


def reference(query, keys_words, keys_scales, lam, bar, reserve, os, vals, hold, offs):
    idx = unstriped(offs)
    keysu = unpack_weight(keys_words, keys_scales, "e2m1")
    keysidxg = keysu[:, idx]
    queryq = mxq(f64(query), 0, "e4m3")
    a0 = keysidxg.T @ queryq
    ag = a0.reshape(I, V, Q // V).mean(axis=2)
    ar = np.repeat(ag, Q // V, axis=1)
    s0 = a0 * f64(lam) - np.square(a0 - ar)
    s = s0.T
    p = np.exp(s)
    pm = p.reshape(Q, G, I // G).mean(axis=2)
    pr = np.repeat(pm, I // G, axis=1)
    r = np.maximum(p - pr * f64(bar), 0.0)
    w = r / (np.sum(r, axis=1, keepdims=True) + f64(reserve))
    wo1 = w * f64(os)
    wt1 = wo1.T
    vt1 = f64(vals)[:, idx].T
    vt1q = mxq(vt1, 0, "e4m3")
    wt1q = mxq(wt1, 0, "e4m3")
    o = vt1q.T @ wt1q
    og = o.reshape(E, K, Q // K).mean(axis=2)
    ogr = np.repeat(og, Q // K, axis=1)
    y = o - ogr * f64(hold)
    words, scales = planes(y)
    return y, words, scales

@@ -1,0 +1,353 @@
+from contextlib import ExitStack
+
+import concourse.mybir as mybir
+
+F32 = mybir.dt.float32
+BF16 = mybir.dt.bfloat16
+I32 = mybir.dt.int32
+U32 = mybir.dt.uint32
+U16 = mybir.dt.uint16
+U8 = mybir.dt.uint8
+FP8X4 = mybir.dt.float8_e4m3fn_x4
+FP4X4 = mybir.dt.float4_e2m1fn_x4
+ALU = mybir.AluOpType
+ACT = mybir.ActivationFunctionType
+AX = mybir.AxisListType
+
+P = 128
+PACK = 4
+D, T, SLOTS, Q, E = 512, 2048, 512, 256, 512
+RUN = 8
+HALVES = 2
+HALF_SLOTS = SLOTS // HALVES
+LIST_ROWS = 16
+
+FLOPS = 2 * D * SLOTS * Q + 2 * SLOTS * E * Q
+
+
+def tile_attend_rowtypical_abovepage_beyondgroupread_pl_kernel(
+    tc, query, keys_words, keys_scales, lam, bar, reserve, slot_factor, vals, hold, offs, out_y, out_words, out_scales
+):
+    nc = tc.nc
+    with ExitStack() as ctx:
+        keep = ctx.enter_context(tc.tile_pool(name="keep", bufs=1))
+        psum = ctx.enter_context(tc.psum_pool(name="psum", bufs=1))
+
+        offsets = keep.tile([P, SLOTS // LIST_ROWS], U16, name="offsets")
+        nc.sync.dma_start(offsets[:], offs)
+
+        lam_col = keep.tile([P, 2], F32, name="lam_col", tag="big0")
+        nc.sync.dma_start(lam_col[:], lam.rearrange("o (p e) -> p (o e)", e=2))
+
+        key_scale_pool = keep.tile([P, T], U8, name="key_scale_pool", tag="big3")
+        nc.vector.memset(key_scale_pool[:].bitcast(I32), 0)
+        for quad in range(4):
+            nc.scalar.dma_start(
+                key_scale_pool[32 * quad : 32 * quad + 4, :].bitcast(I32),
+                keys_scales[0, 4 * quad : 4 * quad + 4, :].bitcast(I32),
+            )
+
+        query_raw = keep.tile([P, PACK, Q], F32, name="query_raw", tag="big1")
+        nc.sync.dma_start(query_raw[:], query.rearrange("(p j) q -> p j q", j=PACK))
+        key_word_pool = keep.tile([P, T], U16, name="key_word_pool", tag="big2")
+        nc.sync.dma_start(key_word_pool[:].bitcast(I32), keys_words[0].bitcast(I32))
+
+        vals_dealt = vals.rearrange("(p j) t -> j p t", j=PACK)
+        val_pool = []
+
+        def load_values(j):
+            pool_j = keep.tile([P, T], F32, name="val_pool%d" % j, tag="big%d" % j)
+            nc.sync.dma_start(pool_j[:], vals_dealt[j])
+            val_pool.append(pool_j)
+
+        def load_column(source, width, name, tag):
+            column = keep.tile([P, width], F32, name=name, tag=tag, align_bytes=64)
+            with nc.allow_non_contiguous_dma(reason="a few values a partition"):
+                nc.sync.dma_start(column[:], source)
+            return column
+
+
+        ones = keep.tile([P, 32], F32, name="ones")
+        nc.vector.memset(ones[:], 1.0)
+        ident = keep.tile([P, P], F32, name="ident")
+        nc.vector.memset(ident[:], 0.0)
+        column_index = keep.tile([P, 32], F32, name="column_index", align_bytes=64)
+        nc.vector.tensor_tensor_scan(column_index[:], ones[:], ones[:], 0.0, ALU.mult, ALU.add)
+        row_index = keep.tile([P, 32], F32, name="row_index", align_bytes=64)
+        nc.vector.transpose(row_index[:], column_index[:])
+        for quad in range(4):
+            part_q = slice(32 * quad, 32 * quad + 32)
+            nc.vector.tensor_tensor(ident[part_q, part_q], column_index[part_q, :], row_index[part_q, :], ALU.is_equal)
+        rows = psum.tile([P, 2, Q], F32, name="rows")
+        for h in range(HALVES):
+            nc.tensor.transpose(rows[:, 0, h * P : (h + 1) * P], lam_col[:, h : h + 1].to_broadcast([P, P]), ident[:])
+        load_values(0)
+
+        query_bf = keep.tile([P, Q, PACK], BF16, name="query_bf", tag="query_bf", align_bytes=64)
+        nc.vector.tensor_copy(out=query_bf[:], in_=query_raw[:].rearrange("p j q -> p q j"))
+        query_codes = keep.tile([P, Q], U32, name="query_codes", align_bytes=64)
+        query_scales = keep.tile([P, Q], U8, name="query_scales", align_bytes=64)
+
+        key_scales = []
+        key_words = []
+
+        def gather_keys(k):
+            cols = slice(k * HALF_SLOTS // LIST_ROWS, (k + 1) * HALF_SLOTS // LIST_ROWS)
+            scales_k = keep.tile([P, HALF_SLOTS], U8, name="key_scales%d" % k, tag="key_scales%d" % k, align_bytes=64)
+            nc.vector.tensor_copy(out=scales_k[:], in_=key_scale_pool[:].indirect(offsets[:, cols]))
+            words_k = keep.tile([P, HALF_SLOTS], U16, name="key_words%d" % k, tag="key_words%d" % k, align_bytes=64)
+            nc.vector.tensor_copy(out=words_k[:], in_=key_word_pool[:].indirect(offsets[:, cols]))
+            key_scales.append(scales_k)
+            key_words.append(words_k)
+
+        nc.vector.quantize_mx(
+            out=query_codes[:].bitcast(FP8X4), scales=query_scales[:], in_=query_bf[:].rearrange("p q j -> p (q j)")
+        )
+        load_values(1)
+        bar_col = load_column(bar.rearrange("(h p) o -> p (h o)", p=P), HALVES, "bar_col", "query_bf")
+        gather_keys(0)
+
+        neg_lam = keep.tile([P, Q], F32, name="neg_lam")
+        nc.scalar.activation(
+            neg_lam[:].rearrange("p (n e) -> p n e", e=2),
+            rows[:, 0, :].rearrange("p (e n) -> p n e", e=2),
+            ACT.Copy,
+            scale=-1.0,
+        )
+        neg_bar = keep.tile([P, HALVES], F32, name="neg_bar")
+        nc.scalar.activation(neg_bar[:], bar_col[:], ACT.Copy, scale=-1.0 / RUN)
+
+        def scores(k):
+            bank = psum.tile([P, 2, Q], F32, name="score%d" % k, tag="product", bufs=2)
+            for c in range(2):
+                cols = slice(c * P, (c + 1) * P)
+                nc.tensor.matmul_mx(
+                    out=bank[:, c, :],
+                    lhsT=key_words[k][:, cols].bitcast(FP4X4),
+                    lhsT_scale=key_scales[k][:, cols],
+                    rhs=query_codes[:].bitcast(FP8X4),
+                    rhs_scale=query_scales[:],
+                    start=True,
+                    stop=True,
+                )
+            return bank
+
+        score = [scores(0)]
+        gather_keys(1)
+        score.append(scores(1))
+
+        factor_col = load_column(slot_factor.rearrange("o (p j) -> p (o j)", j=PACK), PACK, "factor_col", "key_scales0")
+        reserve_col = load_column(reserve.rearrange("(h p) o -> p (h o)", p=P), HALVES, "reserve_col", "key_words0")
+        load_values(2)
+        load_values(3)
+        hold_col = load_column(hold.rearrange("o (h p) -> p (o h)", p=P), HALVES, "hold_col", "key_scales1")
+
+        factor_rows = psum.tile([P, PACK, P], F32, name="factor_rows")
+        for j in range(PACK):
+            nc.tensor.transpose(factor_rows[:, j, :], factor_col[:, j : j + 1].to_broadcast([P, P]), ident[:])
+        for h in range(HALVES):
+            nc.tensor.transpose(rows[:, 1, h * P : (h + 1) * P], hold_col[:, h : h + 1].to_broadcast([P, P]), ident[:])
+
+        groups = 2 * Q // RUN
+
+        def weights_exp(k):
+            bank = score[k]
+            by_group = bank[:].rearrange("p c (v g) -> p (c v) g", g=RUN)
+            group_sum = keep.tile([P, groups], F32, name="group_sum%d" % k)
+            nc.vector.tensor_reduce(out=group_sum[:], in_=by_group, axis=AX.X, op=ALU.add)
+            diff = keep.tile([P, 2, Q], F32, name="diff%d" % k)
+            nc.vector.scalar_tensor_tensor(
+                out=diff[:].rearrange("p c (v g) -> p (c v) g", g=RUN),
+                in0=group_sum[:].unsqueeze(2).to_broadcast([P, groups, RUN]),
+                scalar=-1.0 / RUN,
+                in1=by_group,
+                op0=ALU.mult,
+                op1=ALU.add,
+            )
+            neg_linear = keep.tile([P, 2, Q], F32, name="neg_linear%d" % k)
+            nc.vector.tensor_tensor(
+                out=neg_linear[:], in0=bank[:], in1=neg_lam[:].unsqueeze(1).to_broadcast([P, 2, Q]), op=ALU.mult
+            )
+            square = keep.tile([P, 2, Q], F32, name="square%d" % k)
+            nc.scalar.activation(square[:], diff[:], ACT.Square)
+            turned = psum.tile([P, HALVES, 2, P], F32, name="turned%d" % k, tag="turned", bufs=2)
+            for h in range(HALVES):
+                for c in range(2):
+                    for n, term in enumerate((neg_linear, square)):
+                        nc.tensor.matmul(
+                            turned[:, h, c, :],
+                            lhsT=term[:, c, h * P : (h + 1) * P],
+                            rhs=ident[:],
+                            start=(n == 0),
+                            stop=(n == 1),
+                            is_transpose=True,
+                        )
+            p_k = keep.tile([P, HALVES, HALF_SLOTS], F32, name="p%d" % k)
+            nc.scalar.activation(p_k[:], turned[:].rearrange("p h c n -> p h (c n)"), ACT.Exp, scale=-1.0)
+            return p_k
+
+        val_codes = []
+        val_scales = []
+
+        def values(j, split):
+            picked = keep.tile([P, SLOTS], BF16, name="picked%d" % j)
+            half = HALF_SLOTS // LIST_ROWS
+            nc.scalar.activation(picked[:, :HALF_SLOTS], val_pool[j][:].indirect(offsets[:, :half]), ACT.Copy)
+            if split:
+                nc.vector.tensor_copy(out=picked[:, HALF_SLOTS:], in_=val_pool[j][:].indirect(offsets[:, half:]))
+            else:
+                nc.scalar.activation(picked[:, HALF_SLOTS:], val_pool[j][:].indirect(offsets[:, half:]), ACT.Copy)
+            words = picked[:].bitcast(F32)
+            bank = psum.tile([P, 2, P], F32, name="val_turned%d" % j, tag="val_turned", bufs=2)
+            for u in range(2):
+                nc.tensor.transpose(bank[:, u, :], words[:, u : SLOTS // 2 : 2], ident[:])
+            grouped = keep.tile([P, P, PACK], BF16, name="val_grouped%d" % j, align_bytes=64)
+            nc.scalar.copy(out=grouped[:].bitcast(F32), in_=bank[:].rearrange("p u e -> p e u"))
+            codes = keep.tile([P, P], U32, name="val_codes%d" % j, align_bytes=64)
+            scales = keep.tile([P, P], U8, name="val_scales%d" % j, align_bytes=64)
+            nc.vector.quantize_mx(
+                out=codes[:].bitcast(FP8X4), scales=scales[:], in_=grouped[:].rearrange("p e j -> p (e j)")
+            )
+            val_codes.append(codes)
+            val_scales.append(scales)
+
+        part = keep.tile([P, HALVES, SLOTS], F32, name="part")
+        part_sum = [keep.tile([P, 2], F32, name="part_sum%d" % h) for h in range(HALVES)]
+        runs = HALF_SLOTS // RUN
+
+        def parts(k, p_k):
+            run_sum = keep.tile([P, HALVES, runs], F32, name="run_sum%d" % k)
+            nc.vector.tensor_reduce(
+                out=run_sum[:].rearrange("p h g -> p (h g)"),
+                in_=p_k[:].rearrange("p h (g r) -> p (h g) r", r=RUN),
+                axis=AX.X,
+                op=ALU.add,
+            )
+            for h in range(HALVES):
+                over = keep.tile([P, runs, RUN], F32, name="over%d_%d" % (k, h))
+                nc.vector.scalar_tensor_tensor(
+                    out=over[:],
+                    in0=run_sum[:, h, :].unsqueeze(2).to_broadcast([P, runs, RUN]),
+                    scalar=neg_bar[:, h : h + 1],
+                    in1=p_k[:, h, :].rearrange("p (g r) -> p g r", r=RUN),
+                    op0=ALU.mult,
+                    op1=ALU.add,
+                )
+                nc.scalar.activation(
+                    part[:, h, k * HALF_SLOTS : (k + 1) * HALF_SLOTS],
+                    over[:].rearrange("p g r -> p (g r)"),
+                    ACT.Relu,
+                    accum_out=part_sum[h][:, k : k + 1],
+                )
+
+        p_0 = weights_exp(0)
+        values(0, False)
+        p_1 = weights_exp(1)
+        values(1, False)
+        parts(0, p_0)
+        parts(1, p_1)
+        values(2, False)
+
+        weight_codes = []
+        weight_scales = []
+
+        def weights(h):
+            total = keep.tile([P, 1], F32, name="total%d" % h)
+            nc.vector.scalar_tensor_tensor(
+                out=total[:],
+                in0=part_sum[h][:, 0:1],
+                scalar=reserve_col[:, h : h + 1],
+                in1=part_sum[h][:, 1:2],
+                op0=ALU.add,
+                op1=ALU.add,
+            )
+            inverse = keep.tile([P, 1], F32, name="inverse%d" % h)
+            nc.vector.reciprocal(out=inverse[:], in_=total[:])
+            weight_bf = keep.tile([P, P, PACK], BF16, name="weight_bf%d" % h)
+            nc.vector.scalar_tensor_tensor(
+                out=weight_bf[:],
+                in0=part[:, h, :].rearrange("p (n j) -> p n j", j=PACK),
+                scalar=inverse[:],
+                in1=factor_rows[:].rearrange("p j n -> p n j"),
+                op0=ALU.mult,
+                op1=ALU.mult,
+            )
+            words = weight_bf[:].rearrange("p n j -> p (n j)").bitcast(F32)
+            bank = psum.tile([P, 2, P], F32, name="weight_turned%d" % h, tag="turned", bufs=2)
+            for u in range(2):
+                nc.tensor.transpose(bank[:, u, :], words[:, u : SLOTS // 2 : 2], ident[:])
+            grouped = keep.tile([P, P, PACK], BF16, name="weight_grouped%d" % h, align_bytes=64)
+            nc.scalar.copy(out=grouped[:].bitcast(F32), in_=bank[:].rearrange("p u q -> p q u"))
+            codes = keep.tile([P, P], U32, name="weight_codes%d" % h, align_bytes=64)
+            scales = keep.tile([P, P], U8, name="weight_scales%d" % h, align_bytes=64)
+            nc.vector.quantize_mx(
+                out=codes[:].bitcast(FP8X4), scales=scales[:], in_=grouped[:].rearrange("p q j -> p (q j)")
+            )
+            weight_codes.append(codes)
+            weight_scales.append(scales)
+
+        weights(0)
+        weights(1)
+        values(3, True)
+
+        y_dealt = out_y.rearrange("(p j) q -> p j q", j=PACK)
+        y_codes = keep.tile([P, Q], U32, name="y_codes", align_bytes=64)
+        y_scales = keep.tile([P, Q], U8, name="y_scales", align_bytes=64)
+        words_out = out_words[0].rearrange("p c r -> p (c r)").bitcast(I32)
+        half_groups = P // RUN
+
+        def result(h):
+            cols = slice(h * P, (h + 1) * P)
+            bank = psum.tile([P, PACK, P], F32, name="read%d" % h, tag="product", bufs=2)
+            for j in range(PACK):
+                nc.tensor.matmul_mx(
+                    out=bank[:, j, :],
+                    lhsT=val_codes[j][:].bitcast(FP8X4),
+                    lhsT_scale=val_scales[j][:],
+                    rhs=weight_codes[h][:].bitcast(FP8X4),
+                    rhs_scale=weight_scales[h][:],
+                    start=True,
+                    stop=True,
+                )
+            read_sum = keep.tile([P, PACK, half_groups], F32, name="read_sum%d" % h)
+            nc.vector.tensor_reduce(
+                out=read_sum[:].rearrange("p j v -> p (j v)"),
+                in_=bank[:].rearrange("p j (v g) -> p (j v) g", g=RUN),
+                axis=AX.X,
+                op=ALU.add,
+            )
+            held = keep.tile([P, PACK, half_groups, RUN], F32, name="held%d" % h)
+            nc.vector.tensor_tensor(
+                out=held[:],
+                in0=read_sum[:].unsqueeze(3).to_broadcast([P, PACK, half_groups, RUN]),
+                in1=rows[:, 1, cols].rearrange("p (v g) -> p v g", g=RUN).unsqueeze(1).to_broadcast([P, PACK, half_groups, RUN]),
+                op=ALU.mult,
+            )
+            y = keep.tile([P, PACK, P], F32, name="y%d" % h)
+            nc.vector.scalar_tensor_tensor(
+                out=y[:].rearrange("p j q -> p (j q)"),
+                in0=held[:].rearrange("p j v g -> p (j v g)"),
+                scalar=-1.0 / RUN,
+                in1=bank[:].rearrange("p j q -> p (j q)"),
+                op0=ALU.mult,
+                op1=ALU.add,
+            )
+            nc.sync.dma_start(y_dealt[:, :, cols], y[:])
+            y_bf = keep.tile([P, P, PACK], BF16, name="y_bf%d" % h, align_bytes=64)
+            if h == 0:
+                nc.scalar.copy(out=y_bf[:], in_=y[:].rearrange("p j q -> p q j"))
+            else:
+                nc.vector.tensor_copy(out=y_bf[:], in_=y[:].rearrange("p j q -> p q j"))
+            nc.vector.quantize_mx(
+                out=y_codes[:, cols].bitcast(FP8X4), scales=y_scales[:, cols], in_=y_bf[:].rearrange("p q j -> p (q j)")
+            )
+
+        result(0)
+        result(1)
+        nc.sync.dma_start(words_out, y_codes[:].bitcast(I32))
+        for quad in range(4):
+            queue = nc.scalar if quad % 2 else nc.sync
+            queue.dma_start(
+                out_scales[0, 4 * quad : 4 * quad + 4, :].bitcast(I32),
+                y_scales[32 * quad : 32 * quad + 4, :].bitcast(I32),
+            )

@@ -36,35 +36,38 @@ def tile_attend_rowtypical_abovepage_beyondgroupread_pl_kernel(
         offsets = keep.tile([P, SLOTS // LIST_ROWS], U16, name="offsets")
         nc.sync.dma_start(offsets[:], offs)
 
-        lam_col = keep.tile([P, 2], F32, name="lam_col", tag="big0")
-        nc.sync.dma_start(lam_col[:], lam.rearrange("o (p e) -> p (o e)", e=2))
-
-        key_scale_pool = keep.tile([P, T], U8, name="key_scale_pool", tag="big3")
-        nc.vector.memset(key_scale_pool[:].bitcast(I32), 0)
+        key_scale_pool = keep.tile([P, T], U8, name="key_scale_pool")
+        nc.gpsimd.memset(key_scale_pool[:].bitcast(I32), 0)
+        lam_col = keep.tile([P, 2], F32, name="lam_col")
+        nc.scalar.dma_start(lam_col[:], lam.rearrange("o (p e) -> p (o e)", e=2))
         for quad in range(4):
             nc.scalar.dma_start(
                 key_scale_pool[32 * quad : 32 * quad + 4, :].bitcast(I32),
                 keys_scales[0, 4 * quad : 4 * quad + 4, :].bitcast(I32),
             )
-
-        query_raw = keep.tile([P, PACK, Q], F32, name="query_raw", tag="big1")
-        nc.sync.dma_start(query_raw[:], query.rearrange("(p j) q -> p j q", j=PACK))
-        key_word_pool = keep.tile([P, T], U16, name="key_word_pool", tag="big2")
+        key_word_pool = keep.tile([P, T], U16, name="key_word_pool")
         nc.sync.dma_start(key_word_pool[:].bitcast(I32), keys_words[0].bitcast(I32))
+        query_raw = keep.tile([P, PACK, Q], F32, name="query_raw", tag="query_raw")
+        nc.sync.dma_start(query_raw[:], query.rearrange("(p j) q -> p j q", j=PACK))
 
         vals_dealt = vals.rearrange("(p j) t -> j p t", j=PACK)
         val_pool = []
 
         def load_values(j):
-            pool_j = keep.tile([P, T], F32, name="val_pool%d" % j, tag="big%d" % j)
+            pool_j = keep.tile([P, T], F32, name="val_pool%d" % j, tag="val_pool%d" % j, align_bytes=64)
             nc.sync.dma_start(pool_j[:], vals_dealt[j])
             val_pool.append(pool_j)
 
-        def load_column(source, width, name, tag):
-            column = keep.tile([P, width], F32, name=name, tag=tag, align_bytes=64)
+        def load_column(source, width, name):
+            column = keep.tile([P, width], F32, name=name)
             with nc.allow_non_contiguous_dma(reason="a few values a partition"):
-                nc.sync.dma_start(column[:], source)
+                nc.gpsimd.dma_start(column[:], source)
             return column
+
+        bar_col = load_column(bar.rearrange("(h p) o -> p (h o)", p=P), HALVES, "bar_col")
+        factor_col = load_column(slot_factor.rearrange("o (p j) -> p (o j)", j=PACK), PACK, "factor_col")
+        reserve_col = load_column(reserve.rearrange("(h p) o -> p (h o)", p=P), HALVES, "reserve_col")
+        hold_col = load_column(hold.rearrange("o (p e) -> p (o e)", e=2), 2, "hold_col")
 
 
         ones = keep.tile([P, 32], F32, name="ones")
@@ -73,18 +76,23 @@ def tile_attend_rowtypical_abovepage_beyondgroupread_pl_kernel(
         nc.vector.memset(ident[:], 0.0)
         column_index = keep.tile([P, 32], F32, name="column_index", align_bytes=64)
         nc.vector.tensor_tensor_scan(column_index[:], ones[:], ones[:], 0.0, ALU.mult, ALU.add)
-        row_index = keep.tile([P, 32], F32, name="row_index", align_bytes=64)
+        row_index = keep.tile([P, 32], F32, name="row_index", tag="val_pool0", align_bytes=64)
         nc.vector.transpose(row_index[:], column_index[:])
         for quad in range(4):
             part_q = slice(32 * quad, 32 * quad + 32)
             nc.vector.tensor_tensor(ident[part_q, part_q], column_index[part_q, :], row_index[part_q, :], ALU.is_equal)
-        rows = psum.tile([P, 2, Q], F32, name="rows")
-        for h in range(HALVES):
-            nc.tensor.transpose(rows[:, 0, h * P : (h + 1) * P], lam_col[:, h : h + 1].to_broadcast([P, P]), ident[:])
-        load_values(0)
+        for j in range(PACK):
+            load_values(j)
+        lam_rows = psum.tile([P, 2, P], F32, name="lam_rows", tag="spare2")
+        for e in range(2):
+            nc.tensor.transpose(lam_rows[:, e, :], lam_col[:, e : e + 1].to_broadcast([P, P]), ident[:])
+        neg_lam = keep.tile([P, Q], F32, name="neg_lam")
+        nc.scalar.activation(
+            neg_lam[:].rearrange("p (n e) -> p n e", e=2), lam_rows[:].rearrange("p e n -> p n e"), ACT.Copy, scale=-1.0
+        )
 
         query_bf = keep.tile([P, Q, PACK], BF16, name="query_bf", tag="query_bf", align_bytes=64)
-        nc.vector.tensor_copy(out=query_bf[:], in_=query_raw[:].rearrange("p j q -> p q j"))
+        nc.scalar.copy(out=query_bf[:, :P, :], in_=query_raw[:, :, :P].rearrange("p j q -> p q j"))
         query_codes = keep.tile([P, Q], U32, name="query_codes", align_bytes=64)
         query_scales = keep.tile([P, Q], U8, name="query_scales", align_bytes=64)
 
@@ -93,29 +101,20 @@ def tile_attend_rowtypical_abovepage_beyondgroupread_pl_kernel(
 
         def gather_keys(k):
             cols = slice(k * HALF_SLOTS // LIST_ROWS, (k + 1) * HALF_SLOTS // LIST_ROWS)
-            scales_k = keep.tile([P, HALF_SLOTS], U8, name="key_scales%d" % k, tag="key_scales%d" % k, align_bytes=64)
-            nc.vector.tensor_copy(out=scales_k[:], in_=key_scale_pool[:].indirect(offsets[:, cols]))
-            words_k = keep.tile([P, HALF_SLOTS], U16, name="key_words%d" % k, tag="key_words%d" % k, align_bytes=64)
+            words_k = keep.tile([P, HALF_SLOTS], U16, name="key_words%d" % k, align_bytes=64)
             nc.vector.tensor_copy(out=words_k[:], in_=key_word_pool[:].indirect(offsets[:, cols]))
+            scales_k = keep.tile(
+                [P, HALF_SLOTS], U8, name="key_scales%d" % k, tag=("key_scales0", "query_bf")[k], align_bytes=64
+            )
+            nc.vector.tensor_copy(out=scales_k[:], in_=key_scale_pool[:].indirect(offsets[:, cols]))
             key_scales.append(scales_k)
             key_words.append(words_k)
 
+        gather_keys(0)
+        nc.vector.tensor_copy(out=query_bf[:, P:, :], in_=query_raw[:, :, P:].rearrange("p j q -> p q j"))
         nc.vector.quantize_mx(
             out=query_codes[:].bitcast(FP8X4), scales=query_scales[:], in_=query_bf[:].rearrange("p q j -> p (q j)")
         )
-        load_values(1)
-        bar_col = load_column(bar.rearrange("(h p) o -> p (h o)", p=P), HALVES, "bar_col", "query_bf")
-        gather_keys(0)
-
-        neg_lam = keep.tile([P, Q], F32, name="neg_lam")
-        nc.scalar.activation(
-            neg_lam[:].rearrange("p (n e) -> p n e", e=2),
-            rows[:, 0, :].rearrange("p (e n) -> p n e", e=2),
-            ACT.Copy,
-            scale=-1.0,
-        )
-        neg_bar = keep.tile([P, HALVES], F32, name="neg_bar")
-        nc.scalar.activation(neg_bar[:], bar_col[:], ACT.Copy, scale=-1.0 / RUN)
 
         def scores(k):
             bank = psum.tile([P, 2, Q], F32, name="score%d" % k, tag="product", bufs=2)
@@ -136,17 +135,9 @@ def tile_attend_rowtypical_abovepage_beyondgroupread_pl_kernel(
         gather_keys(1)
         score.append(scores(1))
 
-        factor_col = load_column(slot_factor.rearrange("o (p j) -> p (o j)", j=PACK), PACK, "factor_col", "key_scales0")
-        reserve_col = load_column(reserve.rearrange("(h p) o -> p (h o)", p=P), HALVES, "reserve_col", "key_words0")
-        load_values(2)
-        load_values(3)
-        hold_col = load_column(hold.rearrange("o (h p) -> p (o h)", p=P), HALVES, "hold_col", "key_scales1")
 
-        factor_rows = psum.tile([P, PACK, P], F32, name="factor_rows")
-        for j in range(PACK):
-            nc.tensor.transpose(factor_rows[:, j, :], factor_col[:, j : j + 1].to_broadcast([P, P]), ident[:])
-        for h in range(HALVES):
-            nc.tensor.transpose(rows[:, 1, h * P : (h + 1) * P], hold_col[:, h : h + 1].to_broadcast([P, P]), ident[:])
+        neg_bar = keep.tile([P, HALVES], F32, name="neg_bar", tag="query_raw")
+        nc.scalar.activation(neg_bar[:], bar_col[:], ACT.Copy, scale=-1.0 / RUN)
 
         groups = 2 * Q // RUN
 
@@ -169,17 +160,18 @@ def tile_attend_rowtypical_abovepage_beyondgroupread_pl_kernel(
                 out=neg_linear[:], in0=bank[:], in1=neg_lam[:].unsqueeze(1).to_broadcast([P, 2, Q]), op=ALU.mult
             )
             square = keep.tile([P, 2, Q], F32, name="square%d" % k)
-            nc.scalar.activation(square[:], diff[:], ACT.Square)
+            for c in range(2):
+                nc.scalar.activation(square[:, c, :], diff[:, c, :], ACT.Square)
             turned = psum.tile([P, HALVES, 2, P], F32, name="turned%d" % k, tag="turned", bufs=2)
-            for h in range(HALVES):
+            for n, term in enumerate((neg_linear, square)):
                 for c in range(2):
-                    for n, term in enumerate((neg_linear, square)):
+                    for h in range(HALVES):
                         nc.tensor.matmul(
                             turned[:, h, c, :],
                             lhsT=term[:, c, h * P : (h + 1) * P],
                             rhs=ident[:],
-                            start=(n == 0),
-                            stop=(n == 1),
+                            start=(n, h, c) == (0, 0, 0),
+                            stop=(n, h, c) == (1, 1, 1),
                             is_transpose=True,
                         )
             p_k = keep.tile([P, HALVES, HALF_SLOTS], F32, name="p%d" % k)
@@ -198,7 +190,7 @@ def tile_attend_rowtypical_abovepage_beyondgroupread_pl_kernel(
             else:
                 nc.scalar.activation(picked[:, HALF_SLOTS:], val_pool[j][:].indirect(offsets[:, half:]), ACT.Copy)
             words = picked[:].bitcast(F32)
-            bank = psum.tile([P, 2, P], F32, name="val_turned%d" % j, tag="val_turned", bufs=2)
+            bank = psum.tile([P, 2, P], F32, name="val_turned%d" % j, tag="spare%d" % j)
             for u in range(2):
                 nc.tensor.transpose(bank[:, u, :], words[:, u : SLOTS // 2 : 2], ident[:])
             grouped = keep.tile([P, P, PACK], BF16, name="val_grouped%d" % j, align_bytes=64)
@@ -215,7 +207,7 @@ def tile_attend_rowtypical_abovepage_beyondgroupread_pl_kernel(
         part_sum = [keep.tile([P, 2], F32, name="part_sum%d" % h) for h in range(HALVES)]
         runs = HALF_SLOTS // RUN
 
-        def parts(k, p_k):
+        def run_sums(k, p_k):
             run_sum = keep.tile([P, HALVES, runs], F32, name="run_sum%d" % k)
             nc.vector.tensor_reduce(
                 out=run_sum[:].rearrange("p h g -> p (h g)"),
@@ -223,30 +215,38 @@ def tile_attend_rowtypical_abovepage_beyondgroupread_pl_kernel(
                 axis=AX.X,
                 op=ALU.add,
             )
-            for h in range(HALVES):
-                over = keep.tile([P, runs, RUN], F32, name="over%d_%d" % (k, h))
-                nc.vector.scalar_tensor_tensor(
-                    out=over[:],
-                    in0=run_sum[:, h, :].unsqueeze(2).to_broadcast([P, runs, RUN]),
-                    scalar=neg_bar[:, h : h + 1],
-                    in1=p_k[:, h, :].rearrange("p (g r) -> p g r", r=RUN),
-                    op0=ALU.mult,
-                    op1=ALU.add,
-                )
-                nc.scalar.activation(
-                    part[:, h, k * HALF_SLOTS : (k + 1) * HALF_SLOTS],
-                    over[:].rearrange("p g r -> p (g r)"),
-                    ACT.Relu,
-                    accum_out=part_sum[h][:, k : k + 1],
-                )
+            return run_sum
+
+        def parts(k, h, p_k, run_sum):
+            over = keep.tile([P, runs, RUN], F32, name="over%d_%d" % (k, h))
+            nc.vector.scalar_tensor_tensor(
+                out=over[:],
+                in0=run_sum[:, h, :].unsqueeze(2).to_broadcast([P, runs, RUN]),
+                scalar=neg_bar[:, h : h + 1],
+                in1=p_k[:, h, :].rearrange("p (g r) -> p g r", r=RUN),
+                op0=ALU.mult,
+                op1=ALU.add,
+            )
+            nc.scalar.activation(
+                part[:, h, k * HALF_SLOTS : (k + 1) * HALF_SLOTS],
+                over[:].rearrange("p g r -> p (g r)"),
+                ACT.Relu,
+                accum_out=part_sum[h][:, k : k + 1],
+            )
 
         p_0 = weights_exp(0)
-        values(0, False)
         p_1 = weights_exp(1)
-        values(1, False)
-        parts(0, p_0)
-        parts(1, p_1)
-        values(2, False)
+        values(0, False)
+        sums_0 = run_sums(0, p_0)
+        parts(0, 0, p_0, sums_0)
+        sums_1 = run_sums(1, p_1)
+        parts(1, 0, p_1, sums_1)
+        parts(0, 1, p_0, sums_0)
+        parts(1, 1, p_1, sums_1)
+        values(1, True)
+        factor_rows = psum.tile([P, PACK, P], F32, name="factor_rows", tag="spare1")
+        for j in range(PACK):
+            nc.tensor.transpose(factor_rows[:, j, :], factor_col[:, j : j + 1].to_broadcast([P, P]), ident[:])
 
         weight_codes = []
         weight_scales = []
@@ -288,7 +288,11 @@ def tile_attend_rowtypical_abovepage_beyondgroupread_pl_kernel(
 
         weights(0)
         weights(1)
+        values(2, True)
         values(3, True)
+        hold_rows = psum.tile([P, 2, P], F32, name="hold_rows", tag="spare2")
+        for e in range(2):
+            nc.tensor.transpose(hold_rows[:, e, :], hold_col[:, e : e + 1].to_broadcast([P, P]), ident[:])
 
         y_dealt = out_y.rearrange("(p j) q -> p j q", j=PACK)
         y_codes = keep.tile([P, Q], U32, name="y_codes", align_bytes=64)
@@ -317,10 +321,11 @@ def tile_attend_rowtypical_abovepage_beyondgroupread_pl_kernel(
                 op=ALU.add,
             )
             held = keep.tile([P, PACK, half_groups, RUN], F32, name="held%d" % h)
+            hold_half = hold_rows[:, :, h * P // 2 : (h + 1) * P // 2].rearrange("p e (v n) -> p v n e", n=RUN // 2)
             nc.vector.tensor_tensor(
-                out=held[:],
-                in0=read_sum[:].unsqueeze(3).to_broadcast([P, PACK, half_groups, RUN]),
-                in1=rows[:, 1, cols].rearrange("p (v g) -> p v g", g=RUN).unsqueeze(1).to_broadcast([P, PACK, half_groups, RUN]),
+                out=held[:].rearrange("p j v (n e) -> p j v n e", e=2),
+                in0=read_sum[:].unsqueeze(3).unsqueeze(4).to_broadcast([P, PACK, half_groups, RUN // 2, 2]),
+                in1=hold_half.unsqueeze(1).to_broadcast([P, PACK, half_groups, RUN // 2, 2]),
                 op=ALU.mult,
             )
             y = keep.tile([P, PACK, P], F32, name="y%d" % h)

@@ -25,6 +25,14 @@ LIST_ROWS = 16
 FLOPS = 2 * D * SLOTS * Q + 2 * SLOTS * E * Q
 
 
+def woven(grouped):
+    return grouped.rearrange("p (c i) j -> p c j i", i=4)
+
+
+def by_four(planes):
+    return planes.rearrange("p j (c i) -> p c j i", i=4)
+
+
 def tile_attend_rowtypical_abovepage_beyondgroupread_pl_kernel(
     tc, query, keys_words, keys_scales, lam, bar, reserve, slot_factor, vals, hold, offs, out_y, out_words, out_scales
 ):
@@ -47,28 +55,23 @@ def tile_attend_rowtypical_abovepage_beyondgroupread_pl_kernel(
             )
         key_word_pool = keep.tile([P, T], U16, name="key_word_pool")
         nc.sync.dma_start(key_word_pool[:].bitcast(I32), keys_words[0].bitcast(I32))
-        query_raw = keep.tile([P, PACK, Q], F32, name="query_raw", tag="query_raw")
+        query_raw = keep.tile([P, PACK, Q], F32, name="query_raw")
         nc.sync.dma_start(query_raw[:], query.rearrange("(p j) q -> p j q", j=PACK))
 
         vals_dealt = vals.rearrange("(p j) t -> j p t", j=PACK)
         val_pool = []
 
         def load_values(j):
-            pool_j = keep.tile([P, T], F32, name="val_pool%d" % j, tag="val_pool%d" % j, align_bytes=64)
+            pool_j = keep.tile([P, T], F32, name="val_pool%d" % j, tag="val_pool%d" % j)
             nc.sync.dma_start(pool_j[:], vals_dealt[j])
             val_pool.append(pool_j)
 
-        def load_column(source, width, name):
-            column = keep.tile([P, width], F32, name=name)
-            with nc.allow_non_contiguous_dma(reason="a few values a partition"):
-                nc.gpsimd.dma_start(column[:], source)
-            return column
-
-        bar_col = load_column(bar.rearrange("(h p) o -> p (h o)", p=P), HALVES, "bar_col")
-        factor_col = load_column(slot_factor.rearrange("o (p j) -> p (o j)", j=PACK), PACK, "factor_col")
-        reserve_col = load_column(reserve.rearrange("(h p) o -> p (h o)", p=P), HALVES, "reserve_col")
-        hold_col = load_column(hold.rearrange("o (p e) -> p (o e)", e=2), 2, "hold_col")
-
+        short_rows = keep.tile([P, P], F32, name="short_rows")
+        nc.vector.memset(short_rows[:], 0.0)
+        nc.gpsimd.dma_start(short_rows[0:2, :], bar.rearrange("(h n) o -> h (n o)", n=P))
+        nc.gpsimd.dma_start(short_rows[2:4, :], reserve.rearrange("(h n) o -> h (n o)", n=P))
+        nc.gpsimd.dma_start(short_rows[4:6, :], hold.rearrange("o (h n) -> (o h) n", n=P))
+        nc.gpsimd.dma_start(short_rows[6:10, :], slot_factor.rearrange("o (c n) -> (o c) n", n=P))
 
         ones = keep.tile([P, 32], F32, name="ones")
         nc.vector.memset(ones[:], 1.0)
@@ -76,7 +79,7 @@ def tile_attend_rowtypical_abovepage_beyondgroupread_pl_kernel(
         nc.vector.memset(ident[:], 0.0)
         column_index = keep.tile([P, 32], F32, name="column_index", align_bytes=64)
         nc.vector.tensor_tensor_scan(column_index[:], ones[:], ones[:], 0.0, ALU.mult, ALU.add)
-        row_index = keep.tile([P, 32], F32, name="row_index", tag="val_pool0", align_bytes=64)
+        row_index = keep.tile([P, 32], F32, name="row_index", align_bytes=64)
         nc.vector.transpose(row_index[:], column_index[:])
         for quad in range(4):
             part_q = slice(32 * quad, 32 * quad + 32)
@@ -92,7 +95,7 @@ def tile_attend_rowtypical_abovepage_beyondgroupread_pl_kernel(
         )
 
         query_bf = keep.tile([P, Q, PACK], BF16, name="query_bf", tag="query_bf", align_bytes=64)
-        nc.scalar.copy(out=query_bf[:, :P, :], in_=query_raw[:, :, :P].rearrange("p j q -> p q j"))
+        nc.scalar.copy(out=woven(query_bf[:, :P, :]), in_=by_four(query_raw[:, :, :P]))
         query_codes = keep.tile([P, Q], U32, name="query_codes", align_bytes=64)
         query_scales = keep.tile([P, Q], U8, name="query_scales", align_bytes=64)
 
@@ -111,7 +114,7 @@ def tile_attend_rowtypical_abovepage_beyondgroupread_pl_kernel(
             key_words.append(words_k)
 
         gather_keys(0)
-        nc.vector.tensor_copy(out=query_bf[:, P:, :], in_=query_raw[:, :, P:].rearrange("p j q -> p q j"))
+        nc.vector.tensor_copy(out=woven(query_bf[:, P:, :]), in_=by_four(query_raw[:, :, P:]))
         nc.vector.quantize_mx(
             out=query_codes[:].bitcast(FP8X4), scales=query_scales[:], in_=query_bf[:].rearrange("p q j -> p (q j)")
         )
@@ -135,9 +138,6 @@ def tile_attend_rowtypical_abovepage_beyondgroupread_pl_kernel(
         gather_keys(1)
         score.append(scores(1))
 
-
-        neg_bar = keep.tile([P, HALVES], F32, name="neg_bar", tag="query_raw")
-        nc.scalar.activation(neg_bar[:], bar_col[:], ACT.Copy, scale=-1.0 / RUN)
 
         groups = 2 * Q // RUN
 
@@ -175,7 +175,11 @@ def tile_attend_rowtypical_abovepage_beyondgroupread_pl_kernel(
                             is_transpose=True,
                         )
             p_k = keep.tile([P, HALVES, HALF_SLOTS], F32, name="p%d" % k)
-            nc.scalar.activation(p_k[:], turned[:].rearrange("p h c n -> p h (c n)"), ACT.Exp, scale=-1.0)
+            if k == 0:
+                nc.scalar.activation(p_k[:], turned[:].rearrange("p h c n -> p h (c n)"), ACT.Exp, scale=-1.0)
+            else:
+                for h in range(HALVES):
+                    nc.scalar.activation(p_k[:, h, :], turned[:, h].rearrange("p c n -> p (c n)"), ACT.Exp, scale=-1.0)
             return p_k
 
         val_codes = []
@@ -209,12 +213,18 @@ def tile_attend_rowtypical_abovepage_beyondgroupread_pl_kernel(
 
         def run_sums(k, p_k):
             run_sum = keep.tile([P, HALVES, runs], F32, name="run_sum%d" % k)
-            nc.vector.tensor_reduce(
-                out=run_sum[:].rearrange("p h g -> p (h g)"),
-                in_=p_k[:].rearrange("p h (g r) -> p (h g) r", r=RUN),
-                axis=AX.X,
-                op=ALU.add,
-            )
+            if k == 0:
+                nc.vector.tensor_reduce(
+                    out=run_sum[:].rearrange("p h g -> p (h g)"),
+                    in_=p_k[:].rearrange("p h (g r) -> p (h g) r", r=RUN),
+                    axis=AX.X,
+                    op=ALU.add,
+                )
+            else:
+                for h in range(HALVES):
+                    nc.vector.tensor_reduce(
+                        out=run_sum[:, h, :], in_=p_k[:, h, :].rearrange("p (g r) -> p g r", r=RUN), axis=AX.X, op=ALU.add
+                    )
             return run_sum
 
         def parts(k, h, p_k, run_sum):
@@ -237,6 +247,15 @@ def tile_attend_rowtypical_abovepage_beyondgroupread_pl_kernel(
         p_0 = weights_exp(0)
         p_1 = weights_exp(1)
         values(0, False)
+        short_turned = psum.tile([P, P], F32, name="short_turned", tag="spare0")
+        nc.tensor.transpose(short_turned[:], short_rows[:], ident[:])
+        neg_bar = keep.tile([P, HALVES], F32, name="neg_bar")
+        nc.scalar.activation(neg_bar[:], short_turned[:, 0:2], ACT.Copy, scale=-1.0 / RUN)
+        short_cols = keep.tile([P, 8], F32, name="short_cols")
+        nc.scalar.copy(out=short_cols[:], in_=short_turned[:, 2:10])
+        reserve_col = short_cols[:, 0:2]
+        hold_col = short_cols[:, 2:4]
+        factor_col = short_cols[:, 4:8]
         sums_0 = run_sums(0, p_0)
         parts(0, 0, p_0, sums_0)
         sums_1 = run_sums(1, p_1)
@@ -263,19 +282,21 @@ def tile_attend_rowtypical_abovepage_beyondgroupread_pl_kernel(
             )
             inverse = keep.tile([P, 1], F32, name="inverse%d" % h)
             nc.vector.reciprocal(out=inverse[:], in_=total[:])
-            weight_bf = keep.tile([P, P, PACK], BF16, name="weight_bf%d" % h)
-            nc.vector.scalar_tensor_tensor(
-                out=weight_bf[:],
-                in0=part[:, h, :].rearrange("p (n j) -> p n j", j=PACK),
-                scalar=inverse[:],
-                in1=factor_rows[:].rearrange("p j n -> p n j"),
-                op0=ALU.mult,
-                op1=ALU.mult,
-            )
-            words = weight_bf[:].rearrange("p n j -> p (n j)").bitcast(F32)
+            weight_bf = keep.tile([P, 2, P, 2], BF16, name="weight_bf%d" % h)
+            part_pairs = part[:, h, :].rearrange("p (n u e) -> p u n e", u=2, e=2)
+            factor_pairs = factor_rows[:].rearrange("p c (m u e) -> p u (c m) e", u=2, e=2)
             bank = psum.tile([P, 2, P], F32, name="weight_turned%d" % h, tag="turned", bufs=2)
             for u in range(2):
-                nc.tensor.transpose(bank[:, u, :], words[:, u : SLOTS // 2 : 2], ident[:])
+                nc.vector.scalar_tensor_tensor(
+                    out=weight_bf[:, u],
+                    in0=part_pairs[:, u],
+                    scalar=inverse[:],
+                    in1=factor_pairs[:, u],
+                    op0=ALU.mult,
+                    op1=ALU.mult,
+                )
+                words = weight_bf[:, u].rearrange("p n e -> p (n e)").bitcast(F32)
+                nc.tensor.transpose(bank[:, u, :], words, ident[:])
             grouped = keep.tile([P, P, PACK], BF16, name="weight_grouped%d" % h, align_bytes=64)
             nc.scalar.copy(out=grouped[:].bitcast(F32), in_=bank[:].rearrange("p u q -> p q u"))
             codes = keep.tile([P, P], U32, name="weight_codes%d" % h, align_bytes=64)
@@ -321,11 +342,10 @@ def tile_attend_rowtypical_abovepage_beyondgroupread_pl_kernel(
                 op=ALU.add,
             )
             held = keep.tile([P, PACK, half_groups, RUN], F32, name="held%d" % h)
-            hold_half = hold_rows[:, :, h * P // 2 : (h + 1) * P // 2].rearrange("p e (v n) -> p v n e", n=RUN // 2)
             nc.vector.tensor_tensor(
-                out=held[:].rearrange("p j v (n e) -> p j v n e", e=2),
-                in0=read_sum[:].unsqueeze(3).unsqueeze(4).to_broadcast([P, PACK, half_groups, RUN // 2, 2]),
-                in1=hold_half.unsqueeze(1).to_broadcast([P, PACK, half_groups, RUN // 2, 2]),
+                out=held[:],
+                in0=read_sum[:].unsqueeze(3).to_broadcast([P, PACK, half_groups, RUN]),
+                in1=hold_rows[:, h, :].rearrange("p (v g) -> p v g", g=RUN).unsqueeze(1).to_broadcast([P, PACK, half_groups, RUN]),
                 op=ALU.mult,
             )
             y = keep.tile([P, PACK, P], F32, name="y%d" % h)
@@ -340,9 +360,9 @@ def tile_attend_rowtypical_abovepage_beyondgroupread_pl_kernel(
             nc.sync.dma_start(y_dealt[:, :, cols], y[:])
             y_bf = keep.tile([P, P, PACK], BF16, name="y_bf%d" % h, align_bytes=64)
             if h == 0:
-                nc.scalar.copy(out=y_bf[:], in_=y[:].rearrange("p j q -> p q j"))
+                nc.scalar.copy(out=woven(y_bf[:]), in_=by_four(y[:]))
             else:
-                nc.vector.tensor_copy(out=y_bf[:], in_=y[:].rearrange("p j q -> p q j"))
+                nc.vector.tensor_copy(out=woven(y_bf[:]), in_=by_four(y[:]))
             nc.vector.quantize_mx(
                 out=y_codes[:, cols].bitcast(FP8X4), scales=y_scales[:, cols], in_=y_bf[:].rearrange("p q j -> p (q j)")
             )

@@ -66,12 +66,16 @@ def tile_attend_rowtypical_abovepage_beyondgroupread_pl_kernel(
             nc.sync.dma_start(pool_j[:], vals_dealt[j])
             val_pool.append(pool_j)
 
-        short_rows = keep.tile([P, P], F32, name="short_rows")
-        nc.vector.memset(short_rows[:], 0.0)
-        nc.gpsimd.dma_start(short_rows[0:2, :], bar.rearrange("(h n) o -> h (n o)", n=P))
-        nc.gpsimd.dma_start(short_rows[2:4, :], reserve.rearrange("(h n) o -> h (n o)", n=P))
-        nc.gpsimd.dma_start(short_rows[4:6, :], hold.rearrange("o (h n) -> (o h) n", n=P))
-        nc.gpsimd.dma_start(short_rows[6:10, :], slot_factor.rearrange("o (c n) -> (o c) n", n=P))
+        def load_column(source, width, name):
+            column = keep.tile([P, width], F32, name=name)
+            with nc.allow_non_contiguous_dma(reason="a few values a partition"):
+                nc.gpsimd.dma_start(column[:], source)
+            return column
+
+        bar_col = load_column(bar.rearrange("(h p) o -> p (h o)", p=P), HALVES, "bar_col")
+        reserve_col = load_column(reserve.rearrange("(h p) o -> p (h o)", p=P), HALVES, "reserve_col")
+        factor_col = load_column(slot_factor.rearrange("o (p j) -> p (o j)", j=PACK), PACK, "factor_col")
+        hold_col = load_column(hold.rearrange("o (p e) -> p (o e)", e=2), 2, "hold_col")
 
         ones = keep.tile([P, 32], F32, name="ones")
         nc.vector.memset(ones[:], 1.0)
@@ -146,7 +150,7 @@ def tile_attend_rowtypical_abovepage_beyondgroupread_pl_kernel(
             by_group = bank[:].rearrange("p c (v g) -> p (c v) g", g=RUN)
             group_sum = keep.tile([P, groups], F32, name="group_sum%d" % k)
             nc.vector.tensor_reduce(out=group_sum[:], in_=by_group, axis=AX.X, op=ALU.add)
-            diff = keep.tile([P, 2, Q], F32, name="diff%d" % k)
+            diff = keep.tile([P, 2, Q], F32, name="diff%d" % k, tag="diff%d" % k)
             nc.vector.scalar_tensor_tensor(
                 out=diff[:].rearrange("p c (v g) -> p (c v) g", g=RUN),
                 in0=group_sum[:].unsqueeze(2).to_broadcast([P, groups, RUN]),
@@ -155,7 +159,7 @@ def tile_attend_rowtypical_abovepage_beyondgroupread_pl_kernel(
                 op0=ALU.mult,
                 op1=ALU.add,
             )
-            neg_linear = keep.tile([P, 2, Q], F32, name="neg_linear%d" % k)
+            neg_linear = keep.tile([P, 2, Q], F32, name="neg_linear%d" % k, tag="neg_linear%d" % k)
             nc.vector.tensor_tensor(
                 out=neg_linear[:], in0=bank[:], in1=neg_lam[:].unsqueeze(1).to_broadcast([P, 2, Q]), op=ALU.mult
             )
@@ -174,7 +178,7 @@ def tile_attend_rowtypical_abovepage_beyondgroupread_pl_kernel(
                             stop=(n, h, c) == (1, 1, 1),
                             is_transpose=True,
                         )
-            p_k = keep.tile([P, HALVES, HALF_SLOTS], F32, name="p%d" % k)
+            p_k = keep.tile([P, HALVES, HALF_SLOTS], F32, name="p%d" % k, tag="p%d" % k)
             if k == 0:
                 nc.scalar.activation(p_k[:], turned[:].rearrange("p h c n -> p h (c n)"), ACT.Exp, scale=-1.0)
             else:
@@ -186,7 +190,7 @@ def tile_attend_rowtypical_abovepage_beyondgroupread_pl_kernel(
         val_scales = []
 
         def values(j, split):
-            picked = keep.tile([P, SLOTS], BF16, name="picked%d" % j)
+            picked = keep.tile([P, SLOTS], BF16, name="picked%d" % j, tag=("picked0", "neg_linear1", "p1", "picked3")[j])
             half = HALF_SLOTS // LIST_ROWS
             nc.scalar.activation(picked[:, :HALF_SLOTS], val_pool[j][:].indirect(offsets[:, :half]), ACT.Copy)
             if split:
@@ -208,7 +212,7 @@ def tile_attend_rowtypical_abovepage_beyondgroupread_pl_kernel(
             val_scales.append(scales)
 
         part = keep.tile([P, HALVES, SLOTS], F32, name="part")
-        part_sum = [keep.tile([P, 2], F32, name="part_sum%d" % h) for h in range(HALVES)]
+        total = []
         runs = HALF_SLOTS // RUN
 
         def run_sums(k, p_k):
@@ -237,30 +241,28 @@ def tile_attend_rowtypical_abovepage_beyondgroupread_pl_kernel(
                 op0=ALU.mult,
                 op1=ALU.add,
             )
-            nc.scalar.activation(
-                part[:, h, k * HALF_SLOTS : (k + 1) * HALF_SLOTS],
-                over[:].rearrange("p g r -> p (g r)"),
-                ACT.Relu,
-                accum_out=part_sum[h][:, k : k + 1],
-            )
+            part_kh = part[:, h, k * HALF_SLOTS : (k + 1) * HALF_SLOTS]
+            over_flat = over[:].rearrange("p g r -> p (g r)")
+            part_sum = keep.tile([P, 1], F32, name="part_sum%d_%d" % (k, h))
+            if k == 0:
+                nc.scalar.activation(part_kh, over_flat, ACT.Relu, accum_out=part_sum[:])
+                started = keep.tile([P, 1], F32, name="started%d" % h)
+                nc.scalar.activation(started[:], part_sum[:], ACT.Identity, bias=reserve_col[:, h : h + 1])
+                total.append(started)
+            else:
+                nc.vector.tensor_scalar(part_kh, over_flat, 0.0, total[h][:], ALU.max, ALU.add, accum_out=part_sum[:])
+                total[h] = part_sum
 
         p_0 = weights_exp(0)
         p_1 = weights_exp(1)
         values(0, False)
-        short_turned = psum.tile([P, P], F32, name="short_turned", tag="spare0")
-        nc.tensor.transpose(short_turned[:], short_rows[:], ident[:])
-        neg_bar = keep.tile([P, HALVES], F32, name="neg_bar")
-        nc.scalar.activation(neg_bar[:], short_turned[:, 0:2], ACT.Copy, scale=-1.0 / RUN)
-        short_cols = keep.tile([P, 8], F32, name="short_cols")
-        nc.scalar.copy(out=short_cols[:], in_=short_turned[:, 2:10])
-        reserve_col = short_cols[:, 0:2]
-        hold_col = short_cols[:, 2:4]
-        factor_col = short_cols[:, 4:8]
+        neg_bar = keep.tile([P, HALVES], F32, name="neg_bar", tag="diff0")
+        nc.scalar.activation(neg_bar[:], bar_col[:], ACT.Copy, scale=-1.0 / RUN)
         sums_0 = run_sums(0, p_0)
         parts(0, 0, p_0, sums_0)
+        parts(0, 1, p_0, sums_0)
         sums_1 = run_sums(1, p_1)
         parts(1, 0, p_1, sums_1)
-        parts(0, 1, p_0, sums_0)
         parts(1, 1, p_1, sums_1)
         values(1, True)
         factor_rows = psum.tile([P, PACK, P], F32, name="factor_rows", tag="spare1")
@@ -271,20 +273,11 @@ def tile_attend_rowtypical_abovepage_beyondgroupread_pl_kernel(
         weight_scales = []
 
         def weights(h):
-            total = keep.tile([P, 1], F32, name="total%d" % h)
-            nc.vector.scalar_tensor_tensor(
-                out=total[:],
-                in0=part_sum[h][:, 0:1],
-                scalar=reserve_col[:, h : h + 1],
-                in1=part_sum[h][:, 1:2],
-                op0=ALU.add,
-                op1=ALU.add,
-            )
             inverse = keep.tile([P, 1], F32, name="inverse%d" % h)
-            nc.vector.reciprocal(out=inverse[:], in_=total[:])
+            nc.vector.reciprocal(out=inverse[:], in_=total[h][:])
             weight_bf = keep.tile([P, 2, P, 2], BF16, name="weight_bf%d" % h)
             part_pairs = part[:, h, :].rearrange("p (n u e) -> p u n e", u=2, e=2)
-            factor_pairs = factor_rows[:].rearrange("p c (m u e) -> p u (c m) e", u=2, e=2)
+            factor_pairs = factor_rows[:].rearrange("p (u e) n -> p u n e", u=2)
             bank = psum.tile([P, 2, P], F32, name="weight_turned%d" % h, tag="turned", bufs=2)
             for u in range(2):
                 nc.vector.scalar_tensor_tensor(
@@ -342,10 +335,11 @@ def tile_attend_rowtypical_abovepage_beyondgroupread_pl_kernel(
                 op=ALU.add,
             )
             held = keep.tile([P, PACK, half_groups, RUN], F32, name="held%d" % h)
+            hold_half = hold_rows[:, :, h * P // 2 : (h + 1) * P // 2].rearrange("p e (v n) -> p v n e", n=RUN // 2)
             nc.vector.tensor_tensor(
-                out=held[:],
-                in0=read_sum[:].unsqueeze(3).to_broadcast([P, PACK, half_groups, RUN]),
-                in1=hold_rows[:, h, :].rearrange("p (v g) -> p v g", g=RUN).unsqueeze(1).to_broadcast([P, PACK, half_groups, RUN]),
+                out=held[:].rearrange("p j v (n e) -> p j v n e", e=2),
+                in0=read_sum[:].unsqueeze(3).unsqueeze(4).to_broadcast([P, PACK, half_groups, RUN // 2, 2]),
+                in1=hold_half.unsqueeze(1).to_broadcast([P, PACK, half_groups, RUN // 2, 2]),
                 op=ALU.mult,
             )
             y = keep.tile([P, PACK, P], F32, name="y%d" % h)

@@ -190,7 +190,7 @@ def tile_attend_rowtypical_abovepage_beyondgroupread_pl_kernel(
         val_scales = []
 
         def values(j, split):
-            picked = keep.tile([P, SLOTS], BF16, name="picked%d" % j, tag=("picked0", "neg_linear1", "p1", "picked3")[j])
+            picked = keep.tile([P, SLOTS], BF16, name="picked%d" % j, tag=("picked0", "picked1", "p1", "picked3")[j])
             half = HALF_SLOTS // LIST_ROWS
             nc.scalar.activation(picked[:, :HALF_SLOTS], val_pool[j][:].indirect(offsets[:, :half]), ACT.Copy)
             if split:
@@ -264,7 +264,7 @@ def tile_attend_rowtypical_abovepage_beyondgroupread_pl_kernel(
         sums_1 = run_sums(1, p_1)
         parts(1, 0, p_1, sums_1)
         parts(1, 1, p_1, sums_1)
-        values(1, True)
+        values(1, False)
         factor_rows = psum.tile([P, PACK, P], F32, name="factor_rows", tag="spare1")
         for j in range(PACK):
             nc.tensor.transpose(factor_rows[:, j, :], factor_col[:, j : j + 1].to_broadcast([P, P]), ident[:])
@@ -302,7 +302,7 @@ def tile_attend_rowtypical_abovepage_beyondgroupread_pl_kernel(
 
         weights(0)
         weights(1)
-        values(2, True)
+        values(2, False)
         values(3, True)
         hold_rows = psum.tile([P, 2, P], F32, name="hold_rows", tag="spare2")
         for e in range(2):

from contextlib import ExitStack

import concourse.mybir as mybir

F32 = mybir.dt.float32
BF16 = mybir.dt.bfloat16
I32 = mybir.dt.int32
U32 = mybir.dt.uint32
U16 = mybir.dt.uint16
U8 = mybir.dt.uint8
FP8X4 = mybir.dt.float8_e4m3fn_x4
FP4X4 = mybir.dt.float4_e2m1fn_x4
ALU = mybir.AluOpType
ACT = mybir.ActivationFunctionType
AX = mybir.AxisListType

P = 128
PACK = 4
D, T, SLOTS, Q, E = 512, 2048, 512, 256, 512
RUN = 8
HALVES = 2
HALF_SLOTS = SLOTS // HALVES
LIST_ROWS = 16

FLOPS = 2 * D * SLOTS * Q + 2 * SLOTS * E * Q


def woven(grouped):
    return grouped.rearrange("p (c i) j -> p c j i", i=4)


def by_four(planes):
    return planes.rearrange("p j (c i) -> p c j i", i=4)


def tile_attend_rowtypical_abovepage_beyondgroupread_pl_kernel(
    tc, query, keys_words, keys_scales, lam, bar, reserve, slot_factor, vals, hold, offs, out_y, out_words, out_scales
):
    nc = tc.nc
    with ExitStack() as ctx:
        keep = ctx.enter_context(tc.tile_pool(name="keep", bufs=1))
        psum = ctx.enter_context(tc.psum_pool(name="psum", bufs=1))

        offsets = keep.tile([P, SLOTS // LIST_ROWS], U16, name="offsets")
        nc.sync.dma_start(offsets[:], offs)

        key_scale_pool = keep.tile([P, T], U8, name="key_scale_pool")
        nc.gpsimd.memset(key_scale_pool[:].bitcast(I32), 0)
        lam_col = keep.tile([P, 2], F32, name="lam_col")
        nc.scalar.dma_start(lam_col[:], lam.rearrange("o (p e) -> p (o e)", e=2))
        for quad in range(4):
            nc.scalar.dma_start(
                key_scale_pool[32 * quad : 32 * quad + 4, :].bitcast(I32),
                keys_scales[0, 4 * quad : 4 * quad + 4, :].bitcast(I32),
            )
        key_word_pool = keep.tile([P, T], U16, name="key_word_pool")
        nc.sync.dma_start(key_word_pool[:].bitcast(I32), keys_words[0].bitcast(I32))
        query_raw = keep.tile([P, PACK, Q], F32, name="query_raw")
        nc.sync.dma_start(query_raw[:], query.rearrange("(p j) q -> p j q", j=PACK))

        vals_dealt = vals.rearrange("(p j) t -> j p t", j=PACK)
        val_pool = []

        def load_values(j):
            pool_j = keep.tile([P, T], F32, name="val_pool%d" % j, tag="val_pool%d" % j)
            nc.sync.dma_start(pool_j[:], vals_dealt[j])
            val_pool.append(pool_j)

        def load_column(source, width, name):
            column = keep.tile([P, width], F32, name=name)
            with nc.allow_non_contiguous_dma(reason="a few values a partition"):
                nc.gpsimd.dma_start(column[:], source)
            return column

        bar_col = load_column(bar.rearrange("(h p) o -> p (h o)", p=P), HALVES, "bar_col")
        reserve_col = load_column(reserve.rearrange("(h p) o -> p (h o)", p=P), HALVES, "reserve_col")
        factor_col = load_column(slot_factor.rearrange("o (p j) -> p (o j)", j=PACK), PACK, "factor_col")
        hold_col = load_column(hold.rearrange("o (p e) -> p (o e)", e=2), 2, "hold_col")

        ones = keep.tile([P, 32], F32, name="ones")
        nc.vector.memset(ones[:], 1.0)
        ident = keep.tile([P, P], F32, name="ident")
        nc.vector.memset(ident[:], 0.0)
        column_index = keep.tile([P, 32], F32, name="column_index", align_bytes=64)
        nc.vector.tensor_tensor_scan(column_index[:], ones[:], ones[:], 0.0, ALU.mult, ALU.add)
        row_index = keep.tile([P, 32], F32, name="row_index", align_bytes=64)
        nc.vector.transpose(row_index[:], column_index[:])
        for quad in range(4):
            part_q = slice(32 * quad, 32 * quad + 32)
            nc.vector.tensor_tensor(ident[part_q, part_q], column_index[part_q, :], row_index[part_q, :], ALU.is_equal)
        for j in range(PACK):
            load_values(j)
        lam_rows = psum.tile([P, 2, P], F32, name="lam_rows", tag="spare2")
        for e in range(2):
            nc.tensor.transpose(lam_rows[:, e, :], lam_col[:, e : e + 1].to_broadcast([P, P]), ident[:])
        neg_lam = keep.tile([P, Q], F32, name="neg_lam")
        nc.scalar.activation(
            neg_lam[:].rearrange("p (n e) -> p n e", e=2), lam_rows[:].rearrange("p e n -> p n e"), ACT.Copy, scale=-1.0
        )

        query_bf = keep.tile([P, Q, PACK], BF16, name="query_bf", tag="query_bf", align_bytes=64)
        nc.scalar.copy(out=woven(query_bf[:, :P, :]), in_=by_four(query_raw[:, :, :P]))
        query_codes = keep.tile([P, Q], U32, name="query_codes", align_bytes=64)
        query_scales = keep.tile([P, Q], U8, name="query_scales", align_bytes=64)

        key_scales = []
        key_words = []

        def gather_keys(k):
            cols = slice(k * HALF_SLOTS // LIST_ROWS, (k + 1) * HALF_SLOTS // LIST_ROWS)
            words_k = keep.tile([P, HALF_SLOTS], U16, name="key_words%d" % k, align_bytes=64)
            nc.vector.tensor_copy(out=words_k[:], in_=key_word_pool[:].indirect(offsets[:, cols]))
            scales_k = keep.tile(
                [P, HALF_SLOTS], U8, name="key_scales%d" % k, tag=("key_scales0", "query_bf")[k], align_bytes=64
            )
            nc.vector.tensor_copy(out=scales_k[:], in_=key_scale_pool[:].indirect(offsets[:, cols]))
            key_scales.append(scales_k)
            key_words.append(words_k)

        gather_keys(0)
        nc.vector.tensor_copy(out=woven(query_bf[:, P:, :]), in_=by_four(query_raw[:, :, P:]))
        nc.vector.quantize_mx(
            out=query_codes[:].bitcast(FP8X4), scales=query_scales[:], in_=query_bf[:].rearrange("p q j -> p (q j)")
        )

        def scores(k):
            bank = psum.tile([P, 2, Q], F32, name="score%d" % k, tag="product", bufs=2)
            for c in range(2):
                cols = slice(c * P, (c + 1) * P)
                nc.tensor.matmul_mx(
                    out=bank[:, c, :],
                    lhsT=key_words[k][:, cols].bitcast(FP4X4),
                    lhsT_scale=key_scales[k][:, cols],
                    rhs=query_codes[:].bitcast(FP8X4),
                    rhs_scale=query_scales[:],
                    start=True,
                    stop=True,
                )
            return bank

        score = [scores(0)]
        gather_keys(1)
        score.append(scores(1))


        groups = 2 * Q // RUN

        def weights_exp(k):
            bank = score[k]
            by_group = bank[:].rearrange("p c (v g) -> p (c v) g", g=RUN)
            group_sum = keep.tile([P, groups], F32, name="group_sum%d" % k)
            nc.vector.tensor_reduce(out=group_sum[:], in_=by_group, axis=AX.X, op=ALU.add)
            diff = keep.tile([P, 2, Q], F32, name="diff%d" % k, tag="diff%d" % k)
            nc.vector.scalar_tensor_tensor(
                out=diff[:].rearrange("p c (v g) -> p (c v) g", g=RUN),
                in0=group_sum[:].unsqueeze(2).to_broadcast([P, groups, RUN]),
                scalar=-1.0 / RUN,
                in1=by_group,
                op0=ALU.mult,
                op1=ALU.add,
            )
            neg_linear = keep.tile([P, 2, Q], F32, name="neg_linear%d" % k, tag="neg_linear%d" % k)
            nc.vector.tensor_tensor(
                out=neg_linear[:], in0=bank[:], in1=neg_lam[:].unsqueeze(1).to_broadcast([P, 2, Q]), op=ALU.mult
            )
            square = keep.tile([P, 2, Q], F32, name="square%d" % k)
            for c in range(2):
                nc.scalar.activation(square[:, c, :], diff[:, c, :], ACT.Square)
            turned = psum.tile([P, HALVES, 2, P], F32, name="turned%d" % k, tag="turned", bufs=2)
            for n, term in enumerate((neg_linear, square)):
                for c in range(2):
                    for h in range(HALVES):
                        nc.tensor.matmul(
                            turned[:, h, c, :],
                            lhsT=term[:, c, h * P : (h + 1) * P],
                            rhs=ident[:],
                            start=(n, h, c) == (0, 0, 0),
                            stop=(n, h, c) == (1, 1, 1),
                            is_transpose=True,
                        )
            p_k = keep.tile([P, HALVES, HALF_SLOTS], F32, name="p%d" % k, tag="p%d" % k)
            if k == 0:
                nc.scalar.activation(p_k[:], turned[:].rearrange("p h c n -> p h (c n)"), ACT.Exp, scale=-1.0)
            else:
                for h in range(HALVES):
                    nc.scalar.activation(p_k[:, h, :], turned[:, h].rearrange("p c n -> p (c n)"), ACT.Exp, scale=-1.0)
            return p_k

        val_codes = []
        val_scales = []

        def values(j, split):
            picked = keep.tile([P, SLOTS], BF16, name="picked%d" % j, tag=("picked0", "picked1", "p1", "picked3")[j])
            half = HALF_SLOTS // LIST_ROWS
            nc.scalar.activation(picked[:, :HALF_SLOTS], val_pool[j][:].indirect(offsets[:, :half]), ACT.Copy)
            if split:
                nc.vector.tensor_copy(out=picked[:, HALF_SLOTS:], in_=val_pool[j][:].indirect(offsets[:, half:]))
            else:
                nc.scalar.activation(picked[:, HALF_SLOTS:], val_pool[j][:].indirect(offsets[:, half:]), ACT.Copy)
            words = picked[:].bitcast(F32)
            bank = psum.tile([P, 2, P], F32, name="val_turned%d" % j, tag="spare%d" % j)
            for u in range(2):
                nc.tensor.transpose(bank[:, u, :], words[:, u : SLOTS // 2 : 2], ident[:])
            grouped = keep.tile([P, P, PACK], BF16, name="val_grouped%d" % j, align_bytes=64)
            nc.scalar.copy(out=grouped[:].bitcast(F32), in_=bank[:].rearrange("p u e -> p e u"))
            codes = keep.tile([P, P], U32, name="val_codes%d" % j, align_bytes=64)
            scales = keep.tile([P, P], U8, name="val_scales%d" % j, align_bytes=64)
            nc.vector.quantize_mx(
                out=codes[:].bitcast(FP8X4), scales=scales[:], in_=grouped[:].rearrange("p e j -> p (e j)")
            )
            val_codes.append(codes)
            val_scales.append(scales)

        part = keep.tile([P, HALVES, SLOTS], F32, name="part")
        total = []
        runs = HALF_SLOTS // RUN

        def run_sums(k, p_k):
            run_sum = keep.tile([P, HALVES, runs], F32, name="run_sum%d" % k)
            if k == 0:
                nc.vector.tensor_reduce(
                    out=run_sum[:].rearrange("p h g -> p (h g)"),
                    in_=p_k[:].rearrange("p h (g r) -> p (h g) r", r=RUN),
                    axis=AX.X,
                    op=ALU.add,
                )
            else:
                for h in range(HALVES):
                    nc.vector.tensor_reduce(
                        out=run_sum[:, h, :], in_=p_k[:, h, :].rearrange("p (g r) -> p g r", r=RUN), axis=AX.X, op=ALU.add
                    )
            return run_sum

        def parts(k, h, p_k, run_sum):
            over = keep.tile([P, runs, RUN], F32, name="over%d_%d" % (k, h))
            nc.vector.scalar_tensor_tensor(
                out=over[:],
                in0=run_sum[:, h, :].unsqueeze(2).to_broadcast([P, runs, RUN]),
                scalar=neg_bar[:, h : h + 1],
                in1=p_k[:, h, :].rearrange("p (g r) -> p g r", r=RUN),
                op0=ALU.mult,
                op1=ALU.add,
            )
            part_kh = part[:, h, k * HALF_SLOTS : (k + 1) * HALF_SLOTS]
            over_flat = over[:].rearrange("p g r -> p (g r)")
            part_sum = keep.tile([P, 1], F32, name="part_sum%d_%d" % (k, h))
            if k == 0:
                nc.scalar.activation(part_kh, over_flat, ACT.Relu, accum_out=part_sum[:])
                started = keep.tile([P, 1], F32, name="started%d" % h)
                nc.scalar.activation(started[:], part_sum[:], ACT.Identity, bias=reserve_col[:, h : h + 1])
                total.append(started)
            else:
                nc.vector.tensor_scalar(part_kh, over_flat, 0.0, total[h][:], ALU.max, ALU.add, accum_out=part_sum[:])
                total[h] = part_sum

        p_0 = weights_exp(0)
        p_1 = weights_exp(1)
        values(0, False)
        neg_bar = keep.tile([P, HALVES], F32, name="neg_bar", tag="diff0")
        nc.scalar.activation(neg_bar[:], bar_col[:], ACT.Copy, scale=-1.0 / RUN)
        sums_0 = run_sums(0, p_0)
        parts(0, 0, p_0, sums_0)
        parts(0, 1, p_0, sums_0)
        sums_1 = run_sums(1, p_1)
        parts(1, 0, p_1, sums_1)
        parts(1, 1, p_1, sums_1)
        values(1, False)
        factor_rows = psum.tile([P, PACK, P], F32, name="factor_rows", tag="spare1")
        for j in range(PACK):
            nc.tensor.transpose(factor_rows[:, j, :], factor_col[:, j : j + 1].to_broadcast([P, P]), ident[:])

        weight_codes = []
        weight_scales = []

        def weights(h):
            inverse = keep.tile([P, 1], F32, name="inverse%d" % h)
            nc.vector.reciprocal(out=inverse[:], in_=total[h][:])
            weight_bf = keep.tile([P, 2, P, 2], BF16, name="weight_bf%d" % h)
            part_pairs = part[:, h, :].rearrange("p (n u e) -> p u n e", u=2, e=2)
            factor_pairs = factor_rows[:].rearrange("p (u e) n -> p u n e", u=2)
            bank = psum.tile([P, 2, P], F32, name="weight_turned%d" % h, tag="turned", bufs=2)
            for u in range(2):
                nc.vector.scalar_tensor_tensor(
                    out=weight_bf[:, u],
                    in0=part_pairs[:, u],
                    scalar=inverse[:],
                    in1=factor_pairs[:, u],
                    op0=ALU.mult,
                    op1=ALU.mult,
                )
                words = weight_bf[:, u].rearrange("p n e -> p (n e)").bitcast(F32)
                nc.tensor.transpose(bank[:, u, :], words, ident[:])
            grouped = keep.tile([P, P, PACK], BF16, name="weight_grouped%d" % h, align_bytes=64)
            nc.scalar.copy(out=grouped[:].bitcast(F32), in_=bank[:].rearrange("p u q -> p q u"))
            codes = keep.tile([P, P], U32, name="weight_codes%d" % h, align_bytes=64)
            scales = keep.tile([P, P], U8, name="weight_scales%d" % h, align_bytes=64)
            nc.vector.quantize_mx(
                out=codes[:].bitcast(FP8X4), scales=scales[:], in_=grouped[:].rearrange("p q j -> p (q j)")
            )
            weight_codes.append(codes)
            weight_scales.append(scales)

        weights(0)
        weights(1)
        values(2, False)
        values(3, True)
        hold_rows = psum.tile([P, 2, P], F32, name="hold_rows", tag="spare2")
        for e in range(2):
            nc.tensor.transpose(hold_rows[:, e, :], hold_col[:, e : e + 1].to_broadcast([P, P]), ident[:])

        y_dealt = out_y.rearrange("(p j) q -> p j q", j=PACK)
        y_codes = keep.tile([P, Q], U32, name="y_codes", align_bytes=64)
        y_scales = keep.tile([P, Q], U8, name="y_scales", align_bytes=64)
        words_out = out_words[0].rearrange("p c r -> p (c r)").bitcast(I32)
        half_groups = P // RUN

        def result(h):
            cols = slice(h * P, (h + 1) * P)
            bank = psum.tile([P, PACK, P], F32, name="read%d" % h, tag="product", bufs=2)
            for j in range(PACK):
                nc.tensor.matmul_mx(
                    out=bank[:, j, :],
                    lhsT=val_codes[j][:].bitcast(FP8X4),
                    lhsT_scale=val_scales[j][:],
                    rhs=weight_codes[h][:].bitcast(FP8X4),
                    rhs_scale=weight_scales[h][:],
                    start=True,
                    stop=True,
                )
            read_sum = keep.tile([P, PACK, half_groups], F32, name="read_sum%d" % h)
            nc.vector.tensor_reduce(
                out=read_sum[:].rearrange("p j v -> p (j v)"),
                in_=bank[:].rearrange("p j (v g) -> p (j v) g", g=RUN),
                axis=AX.X,
                op=ALU.add,
            )
            held = keep.tile([P, PACK, half_groups, RUN], F32, name="held%d" % h)
            hold_half = hold_rows[:, :, h * P // 2 : (h + 1) * P // 2].rearrange("p e (v n) -> p v n e", n=RUN // 2)
            nc.vector.tensor_tensor(
                out=held[:].rearrange("p j v (n e) -> p j v n e", e=2),
                in0=read_sum[:].unsqueeze(3).unsqueeze(4).to_broadcast([P, PACK, half_groups, RUN // 2, 2]),
                in1=hold_half.unsqueeze(1).to_broadcast([P, PACK, half_groups, RUN // 2, 2]),
                op=ALU.mult,
            )
            y = keep.tile([P, PACK, P], F32, name="y%d" % h)
            nc.vector.scalar_tensor_tensor(
                out=y[:].rearrange("p j q -> p (j q)"),
                in0=held[:].rearrange("p j v g -> p (j v g)"),
                scalar=-1.0 / RUN,
                in1=bank[:].rearrange("p j q -> p (j q)"),
                op0=ALU.mult,
                op1=ALU.add,
            )
            nc.sync.dma_start(y_dealt[:, :, cols], y[:])
            y_bf = keep.tile([P, P, PACK], BF16, name="y_bf%d" % h, align_bytes=64)
            if h == 0:
                nc.scalar.copy(out=woven(y_bf[:]), in_=by_four(y[:]))
            else:
                nc.vector.tensor_copy(out=woven(y_bf[:]), in_=by_four(y[:]))
            nc.vector.quantize_mx(
                out=y_codes[:, cols].bitcast(FP8X4), scales=y_scales[:, cols], in_=y_bf[:].rearrange("p q j -> p (q j)")
            )

        result(0)
        result(1)
        nc.sync.dma_start(words_out, y_codes[:].bitcast(I32))
        for quad in range(4):
            queue = nc.scalar if quad % 2 else nc.sync
            queue.dma_start(
                out_scales[0, 4 * quad : 4 * quad + 4, :].bitcast(I32),
                y_scales[32 * quad : 32 * quad + 4, :].bitcast(I32),
            )
